import numpy as np, ml_dtypes
CORES = [9,25,41,57]
N = 4
BF = ml_dtypes.bfloat16
W, Q, CAP, ST, RO = 8192, 256, 128, 3, 3
R = np.arange(16)[:, None]
def hashes(path, node, w):
    u = np.add.accumulate(path * w[..., 0:1], axis=-2); v = np.add.accumulate(path * w[..., 1:2], axis=-2)
    return (((u * v) >> 5) + 37 * node[..., None, :]) & (W - 1)
def begin(node, path):
    return {"L": node, "G": node, "F": node, "P": path, "X": path, "O": path, "done": np.zeros(node.shape, bool), "Z": np.zeros_like(path), "V": np.zeros_like(node)}
def step(A, nk, w, s):
    h = hashes(s["P"], s["L"], w)
    key = (np.take_along_axis(A, h.reshape(N, 8, 1, 16 * Q), 3) & 15).reshape(N, 8, 16, 16, Q)
    differ = (key != s["P"][:, :, :, None, :]) & (R <= R.T)[:, :, None]
    m = R + 1; match = np.sum(differ, axis=2) <= (m >> 2)
    best = np.max(np.where(match, m, 0), axis=2)
    at = np.take_along_axis(h, np.maximum(best - 1, 0)[:, :, None, :], 2)
    Z = np.take_along_axis(A, at, 3) >> 4; x = np.take_along_axis(nk, at[:, :, 0], 2); node, kind = x >> 2, x & 3
    live = ~s["done"]; hit = live & (best > 0); miss = live & (best == 0)
    plain, quoted, nodal, value = hit & (kind == 0), hit & (kind == 1), hit & (kind == 2), hit & (kind == 3)
    q_, m_ = quoted[:, :, None], miss[:, :, None]
    new = np.where(R < best[:, :, None], Z, np.where(q_, s["X"], s["P"]))
    return {"P": np.where((plain | quoted | nodal)[:, :, None], new, np.where(m_, s["X"], s["P"])), "X": np.where((quoted | nodal)[:, :, None], new, s["X"]), "O": s["O"],
            "L": np.where(plain | nodal, node, np.where(quoted | miss, s["G"], s["L"])), "G": np.where(nodal, node, s["G"]), "F": s["F"],
            "done": s["done"] | value, "Z": np.where(value[:, :, None], Z, s["Z"]), "V": np.where(value, node, s["V"])}
def finish(A, nk, w, s, t):
    place = hashes(s["O"], s["F"], w)[:, :, 15]; done = s["done"]; d_ = done[:, :, None]
    for a in range(N):
        for g in range(8):
            v = np.flatnonzero(done[a, g]); c, k = np.unique(place[a, g, v], return_index=True); v = v[k]
            A[a, g][:, c] = s["O"][a, g][:, v] + 16 * s["Z"][a, g][:, v]; nk[a, g, c] = 4 * s["V"][a, g, v] + 3
    O = np.where(d_, (s["O"] + s["Z"]) & 15, s["O"]); F = np.where(done, s["V"], s["F"])
    old = {"P": np.where(d_, O, s["P"]), "X": np.where(d_, O, s["X"]), "O": O, "L": np.where(done, F, s["L"]), "G": np.where(done, F, s["G"]), "F": F}
    new = begin(F, O)
    for x in "PXOLGF": new[x] = np.array(old[x])
    for a in range(N):
        q = (a - 1 - t) % N
        for g in range(8):
            mine = np.flatnonzero(~done[a, g])[:CAP]; come = np.flatnonzero(~done[q, g])[:CAP][:len(mine)]
            here, spare = mine[:len(come)], mine[len(come):]
            for x in "PXOLGF": new[x][a, g][..., here] = old[x][q, g][..., come]
            for x, y in (("P", "O"), ("X", "O"), ("L", "F"), ("G", "F")): new[x][a, g][..., spare] = old[y][a, g][..., spare]
    return new
def sym(rng, *shape):
    return np.where(rng.random(shape) < 0.7, rng.integers(0, 3, shape), rng.integers(0, 16, shape))
def start(rng):
    A = (sym(rng, N, 8, 16, W) + 16 * sym(rng, N, 8, 16, W)).astype(np.int32)
    nk = 4 * rng.integers(0, 1024, (N, 8, W)) + rng.choice(np.array([0, 0, 0, 1, 1, 2, 2, 3, 3, 3]), (N, 8, W))
    return A, nk, rng.integers(1, 18, (N, 8, 16, 2)), rng.integers(0, 1024, (N, 8, Q)), sym(rng, N, 8, 16, Q)
def plant(rng, A, nk, w, s, used, share, lens, vals, fam, edge):
    h = hashes(s["P"], s["L"], w)
    for a in range(N):
        for g in range(8):
            lane = np.flatnonzero(~s["done"][a, g] & (rng.random(Q) < share[a, g])); m = rng.choice(lens, lane.size); c = h[a, g, m - 1, lane]
            keep = ~used[a, g, c]; lane, m, c = lane[keep], m[keep], c[keep]; used[a, g, c] = True; n = lane.size
            low = R < m; r = np.where(low, rng.random((16, n)), 2.0); order = np.argsort(np.argsort(r, axis=0), axis=0)
            ch = (m >> 2) + rng.integers(0, 2, n) if edge else (rng.random(n) * ((m >> 2) + 1)).astype(np.int64)
            p = s["P"][a, g][:, lane]; col = A[a, g][:, c]
            key = np.where(low, np.where(order < ch, (p + 1 + rng.integers(0, 15, (16, n))) & 15, p), col & 15)
            z = col >> 4; node = nk[a, g, c] >> 2; kind = np.where(rng.random(n) < vals, 3, nk[a, g, c] & 3)
            other = (lane + fam * rng.integers(0, Q // fam, n)) % Q if fam else rng.integers(0, Q, n)
            lead = (kind == 3) & (rng.random(n) < (0.9 if fam else 0.5)); O = s["O"][a, g]
            z = np.where(lead, (O[:, other] - O[:, lane]) & 15, z); node = np.where(lead, s["F"][a, g, other], node)
            A[a, g][:, c] = key + 16 * z; nk[a, g, c] = 4 * node + kind
def walk(rng, A, nk, w, qn, qp, share, lens, vals=0.0, fam=0, edge=False, used=None):
    s = begin(qn, qp); used = np.zeros((N, 8, W), bool) if used is None else used
    for k in range(ST):
        plant(rng, A, nk, w, s, used, share, lens, vals, fam, edge)
        if k < ST - 1: s = step(A, nk, w, s)
def pack(A, nk, w, qn, qp):
    return {"sen": A.reshape(N, 128, W).astype(np.float32).astype(BF), "nk": nk.astype(np.int32), "wt": np.ascontiguousarray(w.reshape(N, 128, 2)).astype(np.int32),
            "qn": qn.astype(np.int32), "qp": qp.reshape(N, 128, Q).astype(np.float32).astype(BF)}
def setup_inputs(rng):
    A, nk, w, qn, qp = start(rng)
    walk(rng, A, nk, w, qn, qp, rng.choice(np.array([0.3, 0.6, 0.9]), (N, 8)), np.arange(1, 17))
    return pack(A, nk, w, qn, qp)
def setup_inputs_alike(rng):
    A, nk, w, qn, qp = start(rng)
    for a in range(N):
        for g in range(8):
            o = rng.integers(0, 1 if g % 2 == 0 else 3, Q); qn[a, g] = qn[a, g, o]; qp[a, g] = qp[a, g][:, o]
            if g < 6:
                h = hashes(qp[a, g], qn[a, g], w[a, g])[15]; A[a, g][:, h] = qp[a, g] + 16 * (A[a, g][:, h] >> 4); nk[a, g, h] = 4 * (nk[a, g, h] >> 2) + (a + g) % 4
    J = Q // 8; O = rng.integers(0, 16, (N, 16, J)); F = rng.integers(0, 1024, (N, J)); Y = rng.integers(0, 16, (N, 16, J)); E = rng.integers(0, 1024, (N, J))
    for a in range(N):
        b = (a + 1) % N; o = rng.integers(0, J, Q); own = rng.permutation(Q) < Q // 2
        qp[a, 6] = np.where(own, O[a][:, o], O[b][:, o]); qn[a, 6] = np.where(own, F[a, o], F[b, o])
        for path, node, z, to, kind in ((O[b], F[b], Y[b], E[b], 2), (Y[b], E[b], Y[b], E[b], 2), (Y[a], E[a], rng.integers(0, 16, (16, J)), rng.integers(0, 1024, J), 3), (O[a], F[a], np.zeros_like(O[a]), F[a], 3)):
            c = hashes(path, node, w[a, 6])[15]; A[a, 6][:, c] = path + 16 * z; nk[a, 6, c] = 4 * to + kind
    return pack(A, nk, w, qn, qp)
def setup_inputs_ends(rng):
    A, nk, w, qn, qp = start(rng); w[:, 3] = 17; w[:, 4] = 1; used = np.zeros((N, 8, W), bool); used[:, :, 0] = True; used[:, :, W - 1] = True
    nk = np.where(rng.random(nk.shape) < 0.5, 4 * rng.choice(np.array([0, 1023]), nk.shape) + (nk & 3), nk)
    qn = np.where(rng.random(qn.shape) < 0.3, rng.choice(np.array([0, 1023]), qn.shape), qn)
    i3 = np.indices((16, 16, 16)).reshape(3, -1); inv = pow(37, -1, W)
    qn[:, :, 0] = 0; qp[:, :, :, 0] = 0; qn[:, :, 1] = 1023; qp[:, :, :, 1] = 15
    qp[:, :, :, 2:10] = 0; qp[:, 3, :, 10:34] = 15
    for a in range(N):
        for g in range(8):
            A[a, g, :, 0] = 16 * rng.integers(0, 16, 16); nk[a, g, 0] = 4 * (nk[a, g, 0] >> 2) + (a + g) % 4
            z = 1 + rng.permutation(64)[:8]; c = 37 * z; qn[a, g, 2:10] = z
            A[a, g][:, c] = 0; nk[a, g, c] = 4 * rng.integers(0, 1024, 8) + (np.arange(8) + a + g) % 4; used[a, g, c] = True
            if g == 3:
                qn[a, g, 10:34] = rng.permutation(np.arange(1000, 1024)); c = hashes(qp[a, g], qn[a, g], w[a, g])[15, 10:34]
                A[a, g][:, c] = 15 + 16 * rng.integers(0, 16, (16, 24)); nk[a, g, c] = 4 * rng.integers(0, 1024, 24) + 2 + np.arange(24) % 2; used[a, g, c] = True
            u = np.sum(w[a, g, :3, 0:1] * i3, axis=0); v = np.sum(w[a, g, :3, 1:2] * i3, axis=0)
            node = ((W - 1 - ((u * v) >> 5)) * inv) & (W - 1); ok = np.flatnonzero(node < 1024)
            if ok.size:
                k = rng.choice(ok); qp[a, g, :, Q - 1] = 0; qp[a, g, :3, Q - 1] = i3[:, k]; qn[a, g, Q - 1] = node[k]
                A[a, g, :, W - 1] = qp[a, g, :, Q - 1] + 16 * rng.integers(0, 16, 16); nk[a, g, W - 1] = 4 * (nk[a, g, W - 1] >> 2) + (a + g + 1) % 4
    walk(rng, A, nk, w, qn, qp, np.full((N, 8), 0.9), np.array([1, 3, 4, 7, 8, 11, 12, 15, 16]), edge=True, used=used)
    return pack(A, nk, w, qn, qp)
def setup_inputs_room(rng):
    A, nk, w, qn, qp = start(rng); few = rng.random(A.shape) < 0.7
    A = (np.where(few, rng.integers(0, 3, A.shape), rng.integers(0, 8, A.shape)) + 16 * rng.integers(0, 8, A.shape)).astype(np.int32)
    nk = 4 * (nk >> 2) + rng.integers(0, 3, nk.shape); qp = np.where(rng.random(qp.shape) < 0.7, rng.integers(0, 3, qp.shape), rng.integers(0, 8, qp.shape))
    want = rng.choice(np.array([0, 1, CAP - 1, CAP, CAP + 1, Q - 256, Q]), (N, 8)); want[0] = (CAP, CAP + 1, Q, CAP - 1, 1, 0, CAP, CAP); want[1] = (CAP, CAP, 0, CAP + 1, Q, CAP, 1, CAP - 1)
    want[2, 3] = Q - 256; want[2, 5] = 0
    for a in range(N):
        for g in range(8):
            n = Q - int(want[a, g])
            if n == 0: continue
            w[a, g] = rng.integers(5, 18, (1, 2))
            p = rng.integers(8, 16, (16, 4 * Q)); i = rng.integers(0, 15, 4 * Q)
            p[i, np.arange(4 * Q)] = 8 + (p[15] + rng.integers(1, 8, 4 * Q)) % 8; node = rng.integers(0, 1024, 4 * Q); h = hashes(p, node, w[a, g])
            k = np.unique(h[14], return_index=True)[1]; k = k[np.unique(h[15, k], return_index=True)[1]]
            k = np.resize(rng.permutation(k), n); up = rng.permutation(Q)[:n]; c = h[14, k]
            z = np.zeros((16, n), np.int64); gap = p[i[k], k] - p[15, k]; z[15] = gap & 15; z[i[k], np.arange(n)] = (-gap) & 15
            qp[a, g][:, up] = p[:, k]; qn[a, g, up] = node[k]; A[a, g][:, c] = p[:, k] + 16 * z; nk[a, g, c] = 4 * node[k] + 3
    return pack(A, nk, w, qn, qp)
def setup_inputs_spread(rng):
    A, nk, w, qn, qp = start(rng); A = rng.integers(0, 256, A.shape).astype(np.int32); nk = rng.integers(0, 4096, nk.shape)
    w = np.minimum(np.exp2(4.2 * rng.random(w.shape)).astype(np.int64), 17); qn = np.minimum(np.exp2(10 * rng.random(qn.shape)).astype(np.int64) - 1, 1023)
    qp = np.minimum((np.exp2(4.5 * rng.random((N, 8, 1, Q))) * rng.random(qp.shape)).astype(np.int64), 15)
    walk(rng, A, nk, w, qn, qp, np.full((N, 8), 0.7), np.arange(1, 17))
    return pack(A, nk, w, qn, qp)
def setup_inputs_ties(rng):
    A, nk, w, qn, qp = start(rng); fam = Q // 16; w = np.ascontiguousarray(np.broadcast_to(rng.integers(1, 18, (N, 8, 1, 2)), w.shape))
    qn = np.tile(rng.integers(0, 1024, (N, 8, fam)), (1, 1, 16)); base = np.tile(rng.integers(0, 16, (N, 8, 16, fam)), (1, 1, 1, 16))
    i = rng.integers(0, 16, (N, 8, 1, Q)); j = (i + 1 + rng.integers(0, 15, i.shape)) % 16
    qp = np.take_along_axis(base, np.where(R == i, j, np.where(R == j, i, R)), 2)
    walk(rng, A, nk, w, qn, qp, np.full((N, 8), 0.9), np.arange(4, 16), vals=0.8, fam=fam)
    o = np.arange(Q).reshape(16, fam).T.reshape(-1); qn[:, 1::2] = qn[:, 1::2][..., o]; qp[:, 1::2] = qp[:, 1::2][..., o]
    return pack(A, nk, w, qn, qp)
def check_inputs(d):
    bad = []
    for k, hi, lo in (("sen", 255, 0), ("nk", 4095, 0), ("wt", 17, 1), ("qn", 1023, 0), ("qp", 15, 0)):
        x = np.asarray(d[k]).astype(np.float64)
        if not (np.all(x >= lo) and np.all(x <= hi) and np.all(x == np.floor(x))): bad.append("range of " + k)
    return bad
def reference(sen, nk, wt, qn, qp):
    A = sen.astype(np.float32).astype(np.int32).reshape(N, 8, 16, W); kn = nk.astype(np.int64); w = wt.astype(np.int64).reshape(N, 8, 16, 2)
    s = begin(qn.astype(np.int64), qp.astype(np.float32).astype(np.int64).reshape(N, 8, 16, Q))
    for t in range(RO):
        for k in range(ST): s = step(A, kn, w, s)
        s = finish(A, kn, w, s, t)
    return {"yp": np.concatenate([s["P"], s["X"]], axis=3).reshape(N, 128, 2 * Q).astype(np.float32).astype(BF), "yn": np.concatenate([s["L"], s["G"]], axis=2).astype(np.float32)}

import numpy as np
from concourse.mybir import AluOpType as ALU, ActivationFunctionType as AF

W, Q, TW, MISS, DUM = 8192, 256, 8464, 8192, 8208
BIG = float(2 ** 21)
ARR, OWN, RST = (1536, 4096, 0), (512, 3072), 2048
SENCH = ((0, 2048), (2048, 4096), (4096, 6144), (6144, 7168), (7168, 8192))
CFG = {"np": "S", "pv": "V", "streams": ((0, 128, 0), (128, 128, 4)), "bias": [1500, 1500, 0], "low": 0,
       "vs": [[0, 32, 4, 12], [16, 24, 16, 24], [24, 16, 12, 12]], "vcopy": "V", "oh": "S", "ex": [6, 0, 0, 1], "nts": 3,
       "sb": "VSSV", "fin": "SSSS", "look": 0.25, "sq": 2, "vk": 0, "nk": "S", "rn": "S", "xr": "S",
       "cyc": 1.0, "pe": 0.52, "gam": 1.55, "sig": 3.8, "hop": 100.0, "fix": 50.0, "pefix": 20.0}


def _mats():
    def m(*ent):
        a = np.zeros((16, 16))
        for k, j, v in ent:
            a[k, j] = v
        return a
    al = slice(0, 16)
    b0 = {"TRI": None, "ONES": None,
          "C32": m((0, al, 37888), (2, al, 37888), (1, al, 1184), (3, al, 1184), (13, al, -1310720)),
          "QH": m((0, [0, 4, 11], 1)), "QL": m((0, [1, 5, 12], 1))}
    b1 = {}
    for n in ["T%d" % x for x in (12, 11, 10, 9, 8)] + ["S%d" % x for x in (3, 4, 5, 6, 7, 2, 1)] + \
            ["P%d" % x for x in (12, 11, 10, 9, 8)] + ["R%d" % x for x in range(16, 7, -1)]:
        b1[n] = None
    b1["KILL"] = m((10, al, -64))
    b1["C32F"] = m((11, al, 37888), (14, al, 37888), (12, al, 1184), (15, al, 1184), (13, al, -1310720))
    b2 = {"SUF": None, "Y": None, "NM0": m((0, al, 512)), "RNAT": m((8, al, 128), (9, al, 1), (10, al, -8192)),
          "CP": m((2, al, -16), (7, al, -145)), "CX": m((2, al, 16), (7, al, -161)),
          "XA": m((0, al, 16), (2, al, 16), (7, al, -16)), "XB": m((0, al, -16), (2, al, -16)),
          "RN1": m((3, [0, 4], 1), (4, [1, 5], 1), (2, [0, 1], -32), (2, [2, 3], 32), (0, [4, 5], 32), (0, [6, 7], -32),
                   (7, [2, 3, 4, 5], -32), (7, [8, 9], -128), (7, 13, 1), (5, 8, 1), (6, 9, 1), (1, [8, 9], 128), (1, 10, 1)),
          "RN2": m((4, [2, 6], 1), (6, [2, 6], 1), (5, [3, 7], 1), (7, [3, 7], 1), (11, 11, 1), (12, 12, 1), (14, 14, 1), (15, 15, 1))}
    h, l, fh, fl = [0, 4, 11], [1, 5, 12], [2, 6, 14], [3, 7, 15]
    nd1 = np.eye(16); nd1[5, 5] = 0; nd1[6, 6] = 0
    b3 = {"BCV": m((10, al, 512)), "GEM": None, "O16K": None, "NVM": m((13, al, 16384), (10, al, -16384)),
          "ZV": m((10, al, 16), (13, al, -145)),
          "FF": m((0, h, 1), (2, h, 1), (1, l, 1), (3, l, 1), (11, fh, 1), (14, fh, 1), (12, fl, 1), (15, fl, 1),
                  (10, h + l, 32), (13, h + l, -32), (10, fh + fl, -32), (13, 13, 1)),
          "ND1": nd1, "ND2": m((5, 5, 1), (6, 6, 1)),
          "OUT": m(([0, 2], 0, 32), ([1, 3], 0, 1), ([4, 6], 1, 32), ([5, 7], 1, 1))}
    return [b0, b1, b2, b3]


MATS = _mats()
NMS = [len(b) for b in MATS]
POFF = [16 * sum(NMS[:i]) for i in range(5)]
SCRATCH = {"ps": ("psum", [128, 4096], "float32")}
for _dt, _bufs in (
        ("bfloat16", {"SEN": W, "KT": TW, "ZT": TW, "NT": TW, "G": 4096, "EQ": 2304, "ST": 4608, "SB": 1536, "PAT": POFF[4], "REP": POFF[4],
                      "E16": 128, "M0": 128 * NMS[0], "M1": 128 * NMS[1], "M2": 128 * NMS[2], "M3": 128 * NMS[3], "ID": 256, "WM": 512,
                      "NKB": 4096, "QNB": 512, "MM": 256, "NM": 256, "CZ": 256, "NG": 256, "TT": 256, "XR": 256, "ZF": 256, "NP": 256,
                      "ND": 256, "DE": 1024, "EB": 48, "ZVB": 256, "YP": 768}),
        ("float32", {"OF": 128, "CF": 32, "JB": 64, "D0": 256, "MK": 256, "SO": 256, "CT": 96, "DOF": 64, "VV": 256, "UV": 256, "PR": 256,
                     "SC": 256, "PV": 256, "PU": 256, "PB": 512, "PS2": 256, "PT": 32, "PLW": 32, "ES": 256, "ES2": 256, "ES3": 128,
                     "ET": 256, "INV": 512, "CS": 24, "CR": 24, "GE": 256, "YN": 512}),
        ("int32", {"NKI": 512, "NKP": 1536, "WTI": 4, "QNI": 256, "QN2": 512, "CI": 16, "XI": 256, "HI": 256, "PX": 256, "PH": 256}),
        ("uint16", {"DOU": 64, "HU": 256, "AU": 16, "PLU": 16, "EU": 64})):
    for _n, _c in _bufs.items():
        SCRATCH[_n] = ("sbuf", [128, _c], _dt)
NDMA = 18
SEMAPHORES = ["s_" + x for x in ["V", "S", "P", "G", "left"] + ["d%d" % i for i in range(NDMA)] + ["cnt0", "cnt1", "cnt2", "arr0", "arr1", "arr2"]]
WIDE = {"float32": 4, "int32": 4, "bfloat16": 2, "uint16": 2}


def A(name, a, b, step=1, p0=0, p1=128, ps=1):
    return (name, a, b, step, p0, p1, ps)


def PS(bank, a, b, p1=128):
    return A("ps", 512 * bank + a, 512 * bank + b, 1, 0, p1)


def IND(win, off):
    return ("ind", win, off)


def n_of(x):
    if x[0] == "ind":
        return 16 * n_of(x[2])
    return len(range(x[1], x[2], x[3]))


def ap(T, x):
    if not isinstance(x, tuple):
        return x
    if x[0] == "ind":
        return ap(T, x[1]).indirect(ap(T, x[2]))
    name, a, b, step, p0, p1, ps = x
    return T[name][slice(p0, p1, ps) if ps > 1 else slice(p0, p1), slice(a, b, step) if step > 1 else slice(a, b)]


def build(C):
    ops = []
    cur = [0, 0, 0]
    cyc = C["cyc"]

    def add(eng, call, cost, reads, writes, lat=0.0, sem=None):
        rd = []
        for x in reads:
            if isinstance(x, tuple):
                rd += [x[1], x[2]] if x[0] == "ind" else [x]
        wr = []
        for x in writes:
            if x[0] == "ind":
                wr.append(x[1]); rd.append(x[2])
            else:
                wr.append(x)
        ops.append({"e": eng, "call": call, "c": cost, "r": rd, "w": wr, "lat": lat, "sem": sem, "h": cur[0], "k": cur[1], "low": cur[2]})

    def narrow(*xs):
        return all(WIDE[SCRATCH[x[0]][2]] == 2 for x in xs)

    def vcost(out, a, b=None):
        if out[0] == "ind":
            return C["fix"] + n_of(out) * C["sig"] * cyc
        if a[0] == "ind":
            return C["fix"] + n_of(a) * C["gam"] * cyc
        n = n_of(out)
        if b is not None:
            n = n * (1 if "ps" in (a[0], b[0]) else 2)
        elif narrow(out, a):
            n = n / 2
        return max(64, n) * cyc + C["fix"] / 2

    def tt(out, a, b, op):
        add("V", lambda g, T, X: g.vector.tensor_tensor(ap(T, out), ap(T, a), ap(T, b), op), vcost(out, a, b), [a, b], [out])

    def ts(out, a, s1, op0, s2=None, op1=None):
        if op1 is None:
            add("V", lambda g, T, X: g.vector.tensor_scalar(ap(T, out), ap(T, a), ap(T, s1), None, op0), vcost(out, a), [a, s1], [out])
        else:
            add("V", lambda g, T, X: g.vector.tensor_scalar(ap(T, out), ap(T, a), ap(T, s1), ap(T, s2), op0, op1), vcost(out, a), [a, s1, s2], [out])

    def cp(out, a, e="V"):
        if e == "S":
            return act(out, a, AF.Identity)
        add("V", lambda g, T, X: g.vector.tensor_copy(ap(T, out), ap(T, a)), vcost(out, a), [a], [out])

    def ms(out, v):
        add("V", lambda g, T, X: g.vector.memset(ap(T, out), v), vcost(out, out), [], [out])

    def scan(out, d0, d1, op0, op1, first=0.0):
        add("V", lambda g, T, X: g.vector.tensor_tensor_scan(ap(T, out), ap(T, d0), ap(T, d1), ap(T, first), op0, op1), vcost(out, d0), [d0, d1, first], [out])

    def act(out, a, f, bias=0.0, scale=1.0):
        c = n_of(a) * cyc * (C["gam"] if a[0] == "ind" else 1) + C["fix"] * 1.3
        add("S", lambda g, T, X: g.scalar.activation(ap(T, out), ap(T, a), f, bias=ap(T, bias), scale=ap(T, scale)), c, [a, bias, scale], [out])

    def relu(out, a, e):
        if e == "S":
            act(out, a, AF.Relu)
        else:
            ts(out, a, 0.0, ALU.max)

    def mm(out, terms):
        for i, (l, r) in enumerate(terms):
            c = max(64, n_of(r)) * C["pe"] * (4 if SCRATCH[r[0]][2] == "float32" else 1) + C["pefix"]
            add("P", lambda g, T, X, l=l, r=r, i=i: g.tensor.matmul(ap(T, out), ap(T, l), ap(T, r), i == 0, i == len(terms) - 1), c, [l, r], [out])

    def iota(out, pat, base, cm=0):
        if SCRATCH[out[0]][2] == "int32":
            add("G", lambda g, T, X: g.iota(ap(T, out), pat, base, cm), 160 + 2 * n_of(out) * cyc, [], [out])
        else:
            add("G", lambda g, T, X: g.iota(ap(T, out), pat, base, cm, allow_small_or_imprecise_dtypes=True), 160 + 2 * n_of(out) * cyc, [], [out])

    def sel(out, pat, op, fill, base, cm):
        add("G", lambda g, T, X: g.affine_select(ap(T, out), ap(T, out), pat, op, float(fill), base, cm), 210 + 2 * n_of(out) * cyc, [out], [out])

    nd = [0]

    def dma(q, out, src, nbytes):
        s = "d%d" % nd[0]; nd[0] += 1
        rd = [src] if src[0] in SCRATCH else []
        wr = [out] if out[0] in SCRATCH else []
        add(q, lambda g, T, X: (g.sync if q == "Y" else g.scalar).dma_start(ap(T, out), ap(T, src)), 100, rd, wr, lat=2000 + nbytes / 200.0, sem=(s, 16))
        ops[-1]["fifo"] = q

    def mat(n, cols=None):
        if n in ("I", "N16"):
            return A("ID", 0, 128) if n == "I" else A("ID", 128, 256)
        for b in range(4):
            if n in MATS[b]:
                i = list(MATS[b]).index(n); nm = NMS[b]
                if cols is None:
                    return A("M%d" % b, i, 128 * nm, nm)
                return A("M%d" % b, i + cols * nm, 128 * nm, 16 * nm)

    def pc(n):
        for b in range(4):
            if n in MATS[b]:
                return POFF[b] + 16 * list(MATS[b]).index(n)

    def pat(c0, n, step=1):
        return A("PAT", c0, c0 + (n - 1) * step + 1, step, 0, 16)

    def line(c0, cs, n, k0, ks, v, kind="eq"):
        out = pat(c0, n, cs if n > 1 else 1)
        if kind == "eq":
            sel(out, [[-ks, n]], ALU.not_equal, v, -k0, 1)
        elif kind == "lt":
            sel(out, [[-ks, n]], ALU.is_ge, v, -k0, 1)
        else:
            sel(out, [[ks, n]], ALU.is_gt, v, k0, -1)

    def sparse(b):
        ent = {}
        for n, a in MATS[b].items():
            if a is not None:
                for k in range(16):
                    for j in range(16):
                        if a[k, j] != 0:
                            ent[(pc(n) + j, k)] = float(a[k, j])
        left = set(ent)
        while left:
            c0, k0 = min(left)
            best = [(c0, k0)]
            for c1, k1 in sorted(left):
                if c1 > c0 and ent[(c1, k1)] == ent[(c0, k0)]:
                    run = [(c0, k0)]
                    while True:
                        nx = (run[-1][0] + c1 - c0, run[-1][1] + k1 - k0)
                        if nx in ent and ent[nx] == ent[(c0, k0)]:
                            run.append(nx)
                        else:
                            break
                    if len([x for x in run if x in left]) > len([x for x in best if x in left]):
                        best = run
            if len(best) > 1:
                line(c0, best[1][0] - c0, len(best), k0, best[1][1] - k0, ent[(c0, k0)])
            else:
                line(c0, 1, 1, k0, 0, ent[(c0, k0)])
            left -= set(best)

    def expand(b, bank):
        nm = NMS[b]
        for j in range(16):
            mm(PS(bank, j * nm, (j + 1) * nm), [(A("E16", 0, 128, 1, 0, 16), A("PAT", POFF[b] + j, POFF[b + 1], 16, 0, 16))])
        rep = A("REP", POFF[b], POFF[b + 1])
        cp(rep, PS(bank, 0, 16 * nm), "S")
        for gg in range(8):
            out = A("M%d" % b, gg * 16 * nm, (gg + 1) * 16 * nm)
            if gg < C["ex"][b]:
                act(out, rep, AF.Identity, scale=A("CF", 8 + gg, 9 + gg))
            else:
                ts(out, rep, A("CF", 8 + gg, 9 + gg), ALU.mult)

    def own(t, h, i):
        a = OWN[t % 2] + 512 * h + 128 * i
        return A("ST", a, a + 128)

    def hf(n, h, o=0):
        return A(n, o + 128 * h, o + 128 * h + 128)

    kcol, fix, theta = A("CF", 0, 1), A("CF", 1, 2), A("CF", 2, 3)
    dma("Y", A("WTI", 0, 2), A("wt", 0, 2), 4096)
    ms(A("QNI", 0, 256), 0)
    ms(A("PAT", 0, POFF[4]), 0.0)
    ms(A("E16", 0, 128), 0.0)
    dma("Y", A("SEN", *SENCH[0]), A("sen", *SENCH[0]), 1 << 19)
    dma("Y", A("QNI", 0, 256, 1, 0, 128, 16), A("qn", 0, 256, 1, 0, 8), 8192)
    dma("S", A("YP", 0, 256), A("qp", 0, 256), 65536)
    dma("S", A("NKI", 0, 512), A("nk", 0, W, 1, 0, 8), 1 << 18)
    for a, b in SENCH[1:]:
        dma("Y", A("SEN", a, b), A("sen", a, b), 256 * b)
    ms(A("ID", 0, 256), 0.0)
    iota(A("CI", 0, 1), [[0, 1]], 0, 1)
    sel(mat("I"), [[-1, 128]], ALU.not_equal, 1, 0, 1)
    sel(mat("N16"), [[-1, 128]], ALU.not_equal, -16, 0, 1)
    sel(A("E16", 0, 128, 1, 0, 16), [[0, 8], [-1, 16]], ALU.not_equal, 1, 0, 1)
    ts(A("CI", 1, 2), A("CI", 0, 1), 15, ALU.bitwise_and)
    ts(A("CI", 2, 3), A("CI", 0, 1), 4, ALU.arith_shift_right)
    cp(A("CF", 0, 1), A("CI", 1, 2))
    cp(A("CF", 3, 4), A("CI", 2, 3))
    iota(A("CF", 16, 24), [[1, 8]], 0)
    ts(A("CF", 8, 16), A("CF", 16, 24), A("CF", 3, 4), ALU.is_equal)
    line(pc("TRI"), 1, 16, 1, 1, 1, "lt")
    ms(pat(pc("ONES"), 16), 1.0)
    sparse(0)
    expand(0, 0)
    cp(A("CF", 24, 26), A("WTI", 0, 2))
    for i, (n, c) in enumerate((("TRI", 24), ("TRI", 25), ("ONES", 24), ("ONES", 25))):
        ts(A("WM", 128 * i, 128 * i + 128), mat(n), A("CF", c, c + 1), ALU.mult)
    ms(A("NT", 0, 1024), 1.0)
    for i in range(1, 8):
        if i <= C["nts"]:
            cp(A("NT", 1024 * i, 1024 * i + 1024), A("NT", 0, 1024), "S")
        else:
            ms(A("NT", 1024 * i, 1024 * i + 1024), 1.0)
    ms(A("NT", W, TW), 1.0)
    ts(A("QN2", 0, 256), A("QNI", 0, 256), 5, ALU.arith_shift_right)
    ts(A("QN2", 256, 512), A("QNI", 0, 256), 31, ALU.bitwise_and)
    cp(A("QNB", 0, 512), A("QN2", 0, 512))
    ts(A("CF", 4, 5), kcol, 13.0, ALU.is_equal)
    mm(PS(1, 0, 256), [(mat("QH"), A("QNB", 0, 256)), (mat("QL"), A("QNB", 256, 512))])
    for h in range(2):
        act(own(0, h, 2), PS(1, 128 * h, 128 * h + 128), AF.Identity, bias=A("CF", 4, 5))
        for i in (0, 1, 3):
            cp(own(0, h, i), hf("YP", h))
    for a in range(0, W, 1024):
        ts(A("ZT", a, a + 1024), A("SEN", a, a + 1024), 0.0625, ALU.mult, 128.53125, ALU.add)
        bk = 4 + 2 * ((a // 1024) % 2)
        for s in range(2):
            c = a + 512 * s
            mm(PS(bk + s, 0, 512), [(mat("I"), A("SEN", c, c + 512)), (mat("N16"), A("ZT", c, c + 512))])
        if a // 1024 >= 8 - C["vk"]:
            act(A("KT", a, a + 512), PS(bk, 0, 512), AF.Identity, bias=2064.0)
            ts(A("KT", a + 512, a + 1024), PS(bk + 1, 0, 512), 2064.0, ALU.add)
        else:
            act(A("KT", a, a + 1024), PS(bk, 0, 1024), AF.Identity, bias=2064.0)
    ms(A("ZT", W, TW), 129.0); ms(A("KT", W, TW), 0.0)
    c = pc("T12")
    sel(pat(c, 80), [[0, 5], [-1, 16]], ALU.not_equal, 1, 0, 1); sel(pat(c, 80), [[-1, 5], [-1, 16]], ALU.is_gt, 0, 12, 0)
    sel(pat(pc("S3"), 80), [[-1, 5], [-1, 16]], ALU.not_equal, 1, 13, 1)
    line(pc("S2") + 11, 1, 2, 0, 1, 1); line(pc("S1") + 10, 1, 1, 0, 0, 1)
    c = pc("P12")
    sel(pat(c, 80), [[0, 5], [-1, 16]], ALU.not_equal, -1, 0, 1); sel(pat(c, 80), [[-1, 5], [-1, 16]], ALU.is_gt, 0, 12, 0)
    sel(pat(c, 64), [[-1, 4], [-1, 16]], ALU.not_equal, -1, 12, 1)
    c = pc("P8")
    line(c + 13, 1, 3, 0, 1, -1); line(c + 11, 1, 2, 0, 1, -1); line(c + 10, 1, 1, 0, 0, -1)
    line(pc("R16") + 15, 15, 9, 16, -1, 1, "lt"); line(pc("R12") + 3, 17, 4, 12, -1, 1, "ge")
    c = pc("R8")
    line(c + 2, 1, 1, 13, 0, 1, "ge"); line(c, 1, 2, 10, 1, 1); line(c + 1, 1, 1, 12, 0, 1)
    sparse(1)
    expand(1, 2)
    line(pc("SUF"), 1, 16, 0, 1, -16, "ge"); line(pc("Y"), 1, 16, 1, 1, -16, "ge"); line(pc("Y"), 1, 16, 0, 1, 1)
    sparse(2)
    expand(2, 3)
    cp(A("OF", 0, 128), mat("ONES"), "S")
    ts(A("NKP", 0, 512), A("NKI", 0, 512), 7, ALU.arith_shift_right)
    ts(A("NKP", 512, 1024), A("NKI", 0, 512), 2, ALU.arith_shift_right, 31, ALU.bitwise_and)
    ts(A("NKP", 1024, 1536), A("NKI", 0, 512), 3, ALU.bitwise_and)
    cp(A("NKB", 1536, 3072), A("NKP", 0, 1536))
    for r, v in enumerate((2.0, 3.0, 1.0)):
        ts(A("NKB", 512 * r, 512 * r + 512), A("NKB", 2560, 3072), v, ALU.is_equal)
    iota(A("NKB", 3584, 3712), [[1, 128]], 0)
    cp(A("NKB", 3712, 3840), A("NKB", 3584, 3712), "S")
    cp(A("NKB", 3840, 4096), A("NKB", 3584, 3840), "S")
    ts(A("CF", 5, 6), kcol, 4.0, ALU.mult)
    ts(A("CF", 28, 32), A("CF", 16, 20), A("CF", 5, 6), ALU.add)
    for j in range(4):
        act(A("NKB", 3072 + 128 * j, 3200 + 128 * j), A("NKB", 3584, 3712), AF.Identity, bias=A("CF", 28 + j, 29 + j), scale=0.0)
    for r, c in enumerate((0, 512, 1024, 1536, 2048, 3072, 3584)):
        dma("Y", A("NT", 0, W, 1, r, 128, 16), A("NKB", c, c + 512), 1 << 17)
    ts(A("NT", MISS, MISS + 1), kcol, 2.0, ALU.is_ge)
    ts(fix, kcol, 15.0, ALU.is_lt, BIG, ALU.mult)
    ts(A("CF", 6, 7), fix, -66048.0, ALU.add)
    ts(A("CF", 7, 8), fix, -512.0, ALU.add)
    ts(A("CI", 3, 4), A("CI", 1, 2), 1.0, ALU.add)
    ts(A("CI", 4, 5), A("CI", 3, 4), 2, ALU.arith_shift_right)
    tt(theta, A("CI", 3, 4), A("CI", 4, 5), ALU.subtract)
    iota(A("JB", 0, 16), [[1, 16]], 0)
    ts(A("JB", 16, 32), A("JB", 0, 16), kcol, ALU.is_equal, 4 * BIG, ALU.mult)
    ts(A("JB", 32, 48), A("JB", 0, 16), -1.0, ALU.add, kcol, ALU.is_equal)
    ts(A("JB", 48, 64), A("JB", 32, 48), -BIG, ALU.mult)
    tt(A("D0", 0, 16), A("JB", 16, 32), A("JB", 48, 64), ALU.add)
    for w in (16, 32, 64, 128):
        cp(A("D0", w, 2 * w), A("D0", 0, w), "S")

    def late_constants():
        line(pc("GEM"), 1, 16, 0, 1, -1, "ge")
        ms(pat(pc("O16K"), 16), 16384.0)
        sparse(3)
        expand(3, 2)
        iota(A("SO", 0, 256), [[512, 2], [1, 128]], 0)
        iota(A("CT", 64, 80), [[16, 16]], 0)
        iota(A("CT", 80, 96), [[512, 2], [16, 8]], 0)
        ts(A("CT", 0, 16), A("CT", 64, 80), kcol, ALU.add, float(DUM), ALU.add)
        ts(A("CT", 16, 32), A("CT", 0, 16), fix, ALU.add, float(-DUM - 256), ALU.add)
        ts(A("CT", 32, 48), A("CT", 80, 96), kcol, ALU.add)
        iota(A("DOF", 0, 64), [[-1, 4], [4, 4], [1, 4]], 0)
        sel(A("DOF", 0, 64), [[-1, 4], [0, 4], [1, 4]], ALU.is_ge, 16, 0, 0)
        cp(A("DOU", 0, 64), A("DOF", 0, 64))
        ms(A("PLW", 16, 32), -1.0); ms(A("INV", 0, 512), 0.0); ms(A("EB", 32, 48), 1.0); ms(A("ST", 384, 512), 0.0)

    ts(A("MK", 0, 16), A("JB", 0, 16), kcol, ALU.is_le, 16384.0, ALU.mult)
    for w in (16, 32, 64, 128):
        cp(A("MK", w, 2 * w), A("MK", 0, w), "S")

    def lanes(t, i, l0, n):
        a = OWN[t % 2] + 512 * (l0 // 128) + 128 * i + l0 % 128
        return A("ST", a, a + n)

    def roles(s):
        l0, n, bk = C["streams"][s]
        if n == 128:
            a, b, c, d = bk, bk + 1, bk + 2, bk + 3
            r = {"v": (b, 0), "u": (a, 0), "c": (a, 128), "p": (b, 128), "q0": (c, 0), "q1": (d, 0), "cnt": (a, 256), "y": (c, 384), "suf": (b, 256),
                 "at": (a, 384), "rn": (b, 384), "cp": (c, 0), "cx": (d, 0), "xb": (d, 128), "xa": (c, 128), "pu": (c, 0), "pc": (c, 128), "pv": (d, 0)}
        else:
            a, b = bk, bk + 1
            r = {"v": (b, 0), "u": (a, 0), "c": (a, 64), "p": (b, 64), "q0": (a, 128), "cnt": (b, 128), "y": (a, 448), "suf": (b, 192),
                 "at": (a, 0), "rn": (b, 256), "cp": (a, 64), "cx": (a, 128), "xb": (b, 320), "xa": (a, 192), "pu": (a, 128), "pc": (a, 192), "pv": (b, 384)}
        return l0, n, lambda x, o=0, w=n: PS(r[x][0], r[x][1] + o, r[x][1] + o + w)

    def place(t, s):
        l0, n, R = roles(s)

        def L(name, o=0):
            return A(name, o + l0, o + l0 + n)
        a, b = l0 // 16, (l0 + n) // 16
        mm(R("pv"), [(A("WM", 384, 512), lanes(t, 3, l0, n))])
        mm(R("pu"), [(A("WM", 256, 384), lanes(t, 3, l0, n))])
        mm(R("pc"), [(mat("C32F"), lanes(t, 2, l0, n))])
        cp(L("PV"), R("pv"), C["pv"])
        tt(L("PU"), R("pu"), L("PV"), ALU.mult)
        tt(L("PX"), R("pc"), L("PU"), ALU.add)
        ts(L("PH"), L("PX"), 5, ALU.arith_shift_right, W - 1, ALU.bitwise_and)
        cp(L("PB", 256), L("PH"))
        tt(L("PB"), L("PB", 256), L("MK"), ALU.add)
        scan(L("PS2"), A("D0", 0, n), L("PB", 256), ALU.add, ALU.min)
        ts(A("PT", a, b), A("PS2", l0 + 15, l0 + n, 16), fix, ALU.add)
        ts(A("PT", 16 + a, 16 + b), A("PT", a, b), 1.0, ALU.add)
        cp(A("PLU", a, b), A("PT", a, b))
        cp(L("NP"), IND(A("NT", 0, DUM), A("PLU", a, b)), C["np"])

    SETS = ((12, 4), (11, 5), (10, 6), (9, 7), (8, 3, 2, 1))

    def step(t, k, s):
        l0, n, R = roles(s)
        cur[0], cur[1] = s, k

        def L(name):
            return A(name, l0, l0 + n)
        P, X, RN = lanes(t, 0, l0, n), lanes(t, 1, l0, n), lanes(t, 2, l0, n)
        mm(R("v"), [(A("WM", 128, 256), P)])
        mm(R("u"), [(A("WM", 0, 128), P)])
        mm(R("c"), [(mat("C32"), RN)])
        cp(L("VV"), R("v"), C["vcopy"])
        mm(R("p"), [(mat("I"), P)])
        tt(L("UV"), R("u"), L("VV"), ALU.mult)
        tt(L("XI"), R("c"), L("UV"), ALU.add)
        ts(L("HI"), L("XI"), 5, ALU.arith_shift_right, W - 1, ALU.bitwise_and)
        cp(L("HU"), L("HI"))
        if k == 0 and t < 2:
            cur[2] = 1
            place(t, s)
            cur[2] = 0
        for q in range(n // 64):
            g0 = l0 + 64 * q
            vs = C["vs"][k][g0 // 64]
            cuts = [g0 + (64 - vs) * i // C["sq"] // 2 * 2 for i in range(C["sq"] + 1)]
            for a, e in zip(cuts, cuts[1:]):
                cp(A("G", 16 * a, 16 * e), IND(A("KT", 0, W), A("HU", a, e)), "S")
            if vs:
                cp(A("G", 16 * cuts[-1], 16 * g0 + 1024), IND(A("KT", 0, W), A("HU", cuts[-1], g0 + 64)), "V")

            def gm(m):
                return A("G", 16 * g0 + m - 1, 16 * g0 + 1024, 16)
            e0 = 9 * g0
            for i, ms_ in enumerate(SETS):
                mm(R("q%d" % q, 64 * i, 64),
                   [(mat("P%d" % ms_[0]), lanes(t, 0, g0, 64)), (mat("T%d" % ms_[0]), gm(ms_[0]))] + [(mat("S%d" % m), gm(m)) for m in ms_[1:]])
            for i in range(4):
                tt(A("EQ", e0 + 64 * i, e0 + 64 * i + 64), gm(16 - i), R("p", 64 * q, 64), ALU.is_equal)
            ts(A("EQ", e0 + 256, e0 + 576), R("q%d" % q, 0, 320), 0.0, ALU.is_equal)
            terms = [(mat("R%d" % (16 - i)), A("EQ", e0 + 64 * i, e0 + 64 * i + 64)) for i in range(9)]
            if k > 0:
                terms = [(mat("KILL"), lanes(t, 2, g0, 64))] + terms
            mm(R("cnt", 64 * q, 64), terms)
        ts(L("MM"), R("cnt"), theta, ALU.is_ge)
        mm(R("y"), [(mat("Y"), L("MM"))])
        mm(R("suf"), [(mat("SUF"), L("MM"))])
        relu(R("y"), R("y"), C["oh"])
        ts(L("NM"), R("suf"), 145.0, ALU.add, 129.0, ALU.max)
        tt(L("PR"), R("y"), L("HI"), ALU.mult)
        mm(R("at"), ([(mat("RNAT"), RN)] if k > 0 else []) + [(mat("NM0"), L("NM")), (A("OF", 0, 128), L("PR"))])
        scan(L("SC"), A("D0", 0, n), R("at"), ALU.add, ALU.min)
        au = A("AU", l0 // 16, (l0 + n) // 16)
        ts(au, A("SC", l0 + 15, l0 + n, 16), A("CF", 6, 7), ALU.add)
        cp(L("NG"), IND(A("NT", 0, DUM), au), C["nk"])
        tt(L("CZ"), IND(A("ZT", 0, DUM), au), L("NM"), ALU.subtract)
        mm(R("cp"), [(mat("I"), P), (mat("I"), L("NM")), (mat("CP"), L("NG"))])
        mm(R("cx"), [(mat("I"), X), (mat("I"), L("NM")), (mat("CX"), L("NG"))])
        mm(R("rn"), [(mat("RN2"), RN), (mat("RN1"), L("NG"))])
        relu(RN, R("rn"), C["rn"])
        tt(L("TT"), R("cp"), L("CZ"), ALU.max)
        tt(P, R("cx"), L("TT"), ALU.max)
        if k == 2:
            cp(L("ZF"), IND(A("ZT", 0, DUM), au), "S")
        mm(R("xb"), [(mat("I"), X), (mat("XB"), L("NG"))])
        mm(R("xa"), [(mat("XA"), L("NG")), (mat("I"), P)])
        relu(L("XR"), R("xb"), C["xr"])
        tt(X, R("xa"), L("XR"), ALU.max)

    def remote(t, src, dst, sem, lat):
        add("G", lambda g, T, X: g.remote_dma(ap(T, dst), ap(T, src), T.sem["s_" + sem], T.sem["s_left"], X["pid"][t], X["rid"][t], X["mask"][t]),
            1000, [src], [A("sent" + sem, 0, 1)], lat=lat, sem=("left", 0))
        add("N", None, 0, [A("sent" + sem, 0, 1)], [dst], sem=(sem, -1))

    def E(i):
        return A("ET", 16 * i, 16 * i + 16)

    def end(t):
        na = 4 if t < 2 else 3
        cur[0] = 0
        ob = OWN[t % 2]
        nv, pos = A("EB", 0, 16), E(1)
        for h in range(2):
            def H(name, o):
                return A(name, o + 8 * h, o + 8 * h + 8)
            sc = A("ES", 128 * h + 15, 128 * h + 128, 16)
            mm(PS(4 * h, 0, 128), [(mat("BCV"), own(t, h, 2))])
            scan(hf("ES", h), A("D0", 0, 128), PS(4 * h, 0, 128), ALU.add, ALU.min)
            ts(H("EB", 0), sc, A("CF", 7, 8), ALU.add, -1.0 / 512, ALU.mult)
            scan(H("EB", 16), A("EB", 32, 40), H("EB", 0), ALU.mult, ALU.add, A("EB", 23, 24) if h else 0.0)
            tt(H("ET", 0), sc, H("CT", 16), ALU.add)
            mm(PS(4 * h, 128, 136), [(mat("GEM"), H("EB", 0)), (mat("ONES"), H("EB", 16))])
            if h:
                mm(PS(4, 136, 140), [(mat("ONES"), A("EB", 28, 32))])
            tt(H("ET", 16), PS(4 * h, 128, 136), H("ET", 0), ALU.max)
            cp(H("EU", 0), H("ET", 16))
            cp(IND(A("INV", 0, 512), H("EU", 0)), hf("SO", h))
        ts(A("CS", 8 * t, 8 * t + 4), PS(4, 136, 140), 128.0, ALU.min)
        remote(t, A("CS", 8 * t, 8 * t + 4), A("CR", 8 * t, 8 * t + 4), "cnt%d" % t, 2500)
        scan(A("ES3", 0, 128), A("D0", 0, 128), A("INV", 0, 128), ALU.add, ALU.min)
        ts(A("EU", 16, 24), A("ES3", 15, 128, 16), fix, ALU.add)
        for i in range(na):
            cp(A("SB", 512 * t + 128 * i, 512 * t + 128 * i + 128), IND(A("ST", ob + 128 * i, ob + 1024), A("EU", 16, 24)), C["sb"][i])
        remote(t, A("SB", 512 * t, 512 * t + 128 * na), A("ST", ARR[t], ARR[t] + 128 * na), "arr%d" % t, 4000)
        for h in range(2):
            mm(PS(2, 128 * h, 128 * h + 128), [(mat("ZV"), own(t, h, 2)), (mat("I"), hf("ZF", h))])
            mm(PS(1, 128 * h, 128 * h + 128), [(mat("FF"), own(t, h, 2))])
        act(A("ZVB", 0, 256), PS(2, 0, 256), AF.Relu)
        for h in range(2):
            mm(PS(3, 128 * h, 128 * h + 128), [(mat("I"), own(t, h, 3)), (mat("I"), hf("ZVB", h))])
        ts(A("GE", 0, 256), PS(3, 0, 256), 16.0, ALU.is_ge, -16.0, ALU.mult)
        for h in range(2):
            r = RST + 512 * h
            act(A("ST", r + 256, r + 384), PS(1, 128 * h, 128 * h + 128), AF.Relu)
            tt(A("ST", r, r + 128), PS(3, 128 * h, 128 * h + 128), hf("GE", h), ALU.add)
            cp(A("ST", r + 128, r + 256), A("ST", r, r + 128), "S")
            if t < 2:
                cp(A("ST", r + 384, r + 512), A("ST", r, r + 128), "S")
        lo, hi = min(ob, RST, ARR[t]), max(ob + 1024, RST + 1024, ARR[t] + 512)
        ts(E(2), pos, 128.0, ALU.is_ge, float(ob - RST), ALU.mult)
        ts(E(3), pos, 256.0, ALU.is_ge, float(RST - ob), ALU.mult)
        tt(E(4), E(2), E(3), ALU.add)
        tt(E(5), E(4), A("CT", 32, 48), ALU.add)
        tt(E(6), pos, E(5), ALU.subtract)
        ts(E(7), E(6), float(ARR[t] - RST), ALU.add)
        ts(E(8), pos, A("CR", 8 * t + 3, 8 * t + 4), ALU.is_lt)
        tt(E(9), E(8), E(7), ALU.mult)
        tt(E(10), E(9), E(5), ALU.add)
        ts(A("EU", 32, 48), E(10), float(RST - lo), ALU.add)
        if t < 2:
            tt(E(11), A("PT", 16, 32), nv, ALU.mult)
            tt(A("PLW", 0, 16), A("PT", 0, 16), E(11), ALU.subtract)
            for j in range(4):
                tt(A("DE", 256 * j, 256 * j + 256), IND(A("PLW", 0, 32), A("DOU", 16 * j, 16 * j + 16)),
                   A("PB", 0, 256) if j == 0 else A("PB", 256, 512), ALU.is_equal)
            for h in range(2):
                mm(PS(6, 128 * h, 128 * h + 128), [(mat("NVM"), own(t, h, 2))] + [(mat("O16K"), hf("DE", h, 256 * j)) for j in range(4)])
            mm(PS(5, 0, 256), [(mat("ND1"), A("NG", 0, 256)), (mat("ND2"), A("NP", 0, 256))])
            cp(A("ND", 0, 256), PS(5, 0, 256), "S")
            scan(A("ES2", 0, 256), A("D0", 0, 256), PS(6, 0, 256), ALU.add, ALU.min)
            ts(E(12), A("ES2", 15, 256, 16), fix, ALU.add)
            tt(E(13), E(12), A("CT", 0, 16), ALU.min)
            tt(E(14), E(13), A("PT", 0, 16), ALU.max)
            cp(A("EU", 48, 64), E(14))
            for tab in ("KT", "ZT", "NT"):
                for blk in (3, 2, 1, 0):
                    o = own(t, blk // 2, 3)[1] + 64 * (blk % 2)
                    src = A("ST", o, o + 64) if tab == "KT" else A("ZF" if tab == "ZT" else "ND", 64 * blk, 64 * blk + 64)
                    cp(IND(A(tab, 0, TW), A("EU", 48 + 4 * blk, 52 + 4 * blk)), src)
            for h in range(2):
                for i in range(4):
                    cp(own(t + 1, h, i), IND(A("ST", lo + 128 * i, hi), A("EU", 32 + 8 * h, 40 + 8 * h)), C["fin"][i])
        else:
            for i, e in ((2, "V"), (0, "S"), (1, "V")):
                cp(A("YP", 256 * i, 256 * i + 256), IND(A("ST", lo + 128 * i, hi), A("EU", 32, 48)), e)
            for i in range(2):
                mm(PS(7, 256 * i, 256 * i + 256, 8), [(mat("OUT", i), A("YP", 512, 768))])
            cp(A("YN", 0, 512, 1, 0, 8), PS(7, 0, 512, 8), "S")
            dma("Y", A("yp", 0, 512), A("YP", 0, 512), 1 << 17)
            dma("S", A("yn", 0, 512, 1, 0, 8), A("YN", 0, 512, 1, 0, 8), 1 << 14)

    for t in range(3):
        for k in range(3):
            if t == 0 and k == 2:
                late_constants()
            for h in range(len(C["streams"])):
                step(t, k, h)
        end(t)
    return ops


def depend(ops):
    hist, banks = {}, {}
    for i, o in enumerate(ops):
        dep, after = set(), set()
        acc = [(x, False) for x in o["r"]] + [(x, True) for x in o["w"]]
        for x, wr in acc:
            name, a, b = x[0], x[1], x[2]
            if name == "ps":
                for bk in range(a // 512, (b - 1) // 512 + 1):
                    st = banks.setdefault(bk, [None, [], []])
                    if st[0] != o["e"]:
                        st[0], st[1], st[2] = o["e"], [y[0] for y in st[2]], []
                    dep.update(st[1])
                    for (j, a2, b2, w2) in st[2]:
                        if o["e"] == "P":
                            after.add(j)
                        elif a < b2 and a2 < b and (wr or w2):
                            dep.add(j)
                    st[2].append((i, a, b, wr))
                continue
            for (j, a2, b2, w2, x2) in hist.get(name, ()):
                if a < b2 and a2 < b and (wr or w2):
                    if x[6] > 1 and x2[6] == x[6] and x[4] != x2[4]:
                        continue
                    dep.add(j)
        for x, wr in acc:
            name, a, b = x[0], x[1], x[2]
            if name == "ps":
                continue
            h = hist.setdefault(name, [])
            if wr and x[3] == 1 and x[4] == 0 and x[5] == 128 and x[6] == 1:
                h[:] = [y for y in h if not (a <= y[1] and y[2] <= b)]
            h.append((i, a, b, wr, x))
        if "fifo" in o:
            if o["fifo"] in banks:
                after.add(banks[o["fifo"]])
            banks[o["fifo"]] = i
        dep.discard(i); after.discard(i)
        o["dep"], o["after"] = dep, after


def schedule(ops, C):
    n = len(ops)
    hop = C["hop"]
    kids = [[] for _ in range(n)]
    for i, o in enumerate(ops):
        for j in o["dep"] | o["after"]:
            kids[j].append(i)
    pr = [0.0] * n
    for i in range(n - 1, -1, -1):
        o = ops[i]
        pr[i] = o["c"] + max([pr[k] + (o["lat"] + hop if i in ops[k]["dep"] else 0) for k in kids[i]] + [o["lat"]])
    pr = [pr[i] - C["bias"][ops[i]["k"]] * ops[i]["h"] - C["low"] * ops[i]["low"] for i in range(n)]
    left = [len(o["dep"] | o["after"]) for o in ops]
    rdy = [0.0] * n
    pool = {}
    for i in range(n):
        if left[i] == 0:
            pool.setdefault(ops[i]["e"], []).append(i)
    free = {}
    order, end = [], 0.0
    while len(order) < n:
        pick = None
        for e, lst in pool.items():
            if not lst:
                continue
            now = max(free.get(e, 0.0), min(rdy[i] for i in lst))
            i = max((i for i in lst if rdy[i] <= now), key=lambda i: pr[i])
            soon = [j for j in lst if now < rdy[j] < now + C["look"] * ops[i]["c"] and pr[j] > pr[i] + ops[i]["c"]]
            if soon:
                i = max(soon, key=lambda j: pr[j])
            st = max(now, rdy[i])
            if pick is None or st < pick[0]:
                pick = (st, i, e)
        st, i, e = pick
        pool[e].remove(i)
        o = ops[i]
        o["t"] = st
        free[e] = st + o["c"]
        end = max(end, st + o["c"] + o["lat"])
        order.append(i)
        for k in kids[i]:
            rdy[k] = max(rdy[k], st + o["c"] + (o["lat"] + hop if i in ops[k]["dep"] else 0))
            left[k] -= 1
            if left[k] == 0:
                pool.setdefault(ops[k]["e"], []).append(k)
    return order, end


def plan(C):
    ops = build(C)
    depend(ops)
    order, end = schedule(ops, C)
    seq = {}
    for i in order:
        o = ops[i]
        key = o["sem"][0] if o["sem"] else o["e"]
        seq[key] = seq.get(key, 0) + 1
        o["key"], o["n"] = key, seq[key]
    known, need = {}, set()
    for i in order:
        o = ops[i]
        if o["e"] == "N":
            o["clock"], o["waits"] = {}, []
            continue
        kn = known.setdefault(o["e"], {})
        top = {}
        for j in o["dep"]:
            p = ops[j]
            if p["key"] not in top or ops[top[p["key"]]]["n"] < p["n"]:
                top[p["key"]] = j
        waits = []
        for j in sorted(top.values(), key=lambda j: (-ops[j]["t"], j)):
            p = ops[j]
            if kn.get(p["key"], 0) < p["n"]:
                waits.append(j); need.add(j)
                kn[p["key"]] = p["n"]
                for key, v in p["clock"].items():
                    if kn.get(key, 0) < v:
                        kn[key] = v
        o["waits"], o["clock"] = waits, dict(kn)
    cnt = {}
    for i in order:
        o = ops[i]
        if o["sem"] is None:
            o["inc"] = i in need
            if o["inc"]:
                cnt[o["e"]] = cnt.get(o["e"], 0) + 1
            o["val"] = cnt.get(o["e"], 0)
    return ops, order, cnt, end


_PLAN = {}


def rank_program(g, core, T, topo):
    rank = T.rank_of(core)
    if rank is None:
        return
    if "p" not in _PLAN:
        _PLAN["p"] = plan(CFG)
    ops, order, cnt, _ = _PLAN["p"]
    n = len(T.cores)
    to = [T.cores[(rank + 1 + t) % n] for t in range(3)]
    fro = [T.cores[(rank - 1 - t) % n] for t in range(3)]
    X = {"rid": [topo.addr(d)[0] for d in to], "pid": [topo.addr(d)[1] for d in to], "mask": [topo.mask(core, d) for d in to]}
    queue = {"V": g.vector, "S": g.scalar, "P": g.tensor, "G": g, "Y": g.sync}
    final = dict(cnt)
    for i in order:
        o = ops[i]
        if o["e"] == "N":
            final[o["key"]] = len(topo.engines(fro[int(o["key"][-1])], core))
            continue
        for j in o["waits"]:
            p = ops[j]
            if p["e"] == "N":
                v = len(topo.engines(fro[int(p["key"][-1])], core))
            else:
                v = p["val"] if p["sem"] is None else p["sem"][1]
            queue[o["e"]].wait_ge(T.sem["s_" + p["key"]], v)
        ins = o["call"](g, T, X)
        if o["sem"] is None:
            if o["inc"]:
                ins.then_inc(T.sem["s_" + o["e"]], 1)
        elif o["key"] != "left":
            ins.then_inc(T.sem["s_" + o["key"]], 16)
            final[o["key"]] = 16
    final["left"] = sum(2 * len(topo.engines(core, d)) for d in to)
    for key, v in final.items():
        g.wait_ge(T.sem["s_" + key], v)
